import numpy as np
import ml_dtypes


def mxq(x, axis, fmt="e4m3"):
    dtype, down = {"e4m3": (ml_dtypes.float8_e4m3fn, 7), "e5m2": (ml_dtypes.float8_e5m2, 14)}[fmt]
    v = np.moveaxis(np.asarray(x, np.float32).astype(ml_dtypes.bfloat16).astype(np.float64), axis, -1)
    blocks = v.reshape(v.shape[:-1] + (-1, 32))
    amax = np.abs(blocks).max(-1, keepdims=True)
    byte = np.maximum(np.where(amax > 0, np.frexp(amax)[1] - 1 + 127, 0) - down, 1)
    scale = np.exp2(byte - 127.0)
    codes = (blocks / scale).astype(np.float32).astype(dtype).astype(np.float64)
    return np.moveaxis((codes * scale).reshape(v.shape), -1, axis)


WIDE = False


def mx_kscale(k):
    if not WIDE:
        return np.ones(k)
    levels = np.array([10, -10, 5, -5, 0])
    if k % 512:
        return np.exp2(np.random.permutation(np.resize(levels, k // 32))).repeat(32)
    a = np.empty((k // 512, 16))
    for p in range(k // 512):
        a[p, :8] = np.random.permutation(np.resize(levels, 8))
        for g in range(8):
            far = levels[np.abs(levels - a[p, g]) >= 10]
            a[p, g + 8] = far[np.random.randint(len(far))]
    return np.exp2(a.ravel()).repeat(32)


def f64(x):
    return np.asarray(x).astype(np.float64)


def striped(idx):
    return np.tile(idx.reshape(-1, 16).T, (8, 1)).astype(np.uint16)


def unstriped(offs):
    return offs[:16].T.reshape(-1).astype(np.int64)


E2M1 = np.array([0.0, 0.5, 1.0, 1.5, 2.0, 3.0, 4.0, 6.0, -0.0, -0.5, -1.0, -1.5, -2.0, -3.0, -4.0, -6.0])


def pack_weight(w, fmt):
    k, n = w.shape
    w = f64(np.asarray(w, np.float32).astype(ml_dtypes.bfloat16)).reshape(k // 32, 32, n)
    amax = np.abs(w).max(1)
    if fmt == "e4m3":
        byte = np.frexp(amax)[1] - 1 + 127 - 7
    else:
        mant, ex = np.frexp(amax / 6.0)
        byte = np.where(mant > 0.5, ex, ex - 1) + 127
    byte = np.clip(np.where(amax > 0, byte, 1), 1, 254)
    scaled = (w * np.exp2(127.0 - byte)[:, None, :]).reshape(k, n).astype(np.float32)
    by_word = np.ascontiguousarray(scaled.reshape(k // 512, 128, 4, n).transpose(0, 1, 3, 2))
    if fmt == "e4m3":
        words = by_word.astype(ml_dtypes.float8_e4m3fn).view(np.uint8)
    else:
        c = by_word.astype(ml_dtypes.float4_e2m1fn).view(np.uint8) & 0xF
        words = (c[..., 0::2] | (c[..., 1::2] << 4)).reshape(k // 512, 128, 2 * n)
    return np.ascontiguousarray(words), np.ascontiguousarray(byte.astype(np.uint8).reshape(k // 512, 16, n))


def unpack_weight(words, scales, fmt):
    g, _, n = scales.shape
    words = np.ascontiguousarray(words).reshape(g, 128, n, -1)
    if fmt == "e4m3":
        vals = words.view(ml_dtypes.float8_e4m3fn).astype(np.float64)
    else:
        nib = np.empty((g, 128, n, 4), np.uint8)
        nib[..., 0::2] = words & 0xF
        nib[..., 1::2] = words >> 4
        vals = E2M1[nib]
    vals = vals * np.repeat(np.exp2(scales.astype(np.float64) - 127.0), 8, axis=1)[..., None]
    return vals.transpose(0, 1, 3, 2).reshape(g * 512, n)


def gelu(v):
    return 0.5 * v * (1.0 + np.tanh(np.sqrt(2.0 / np.pi) * (v + 0.044715 * v**3)))


K, H, N, T, S, T3, P = 1024, 1024, 384, 4096, 1024, 2048, 512


def setup_inputs():
    n = np.random.standard_normal
    s = mx_kscale(K)[:, None]
    u = mx_kscale(H)[:, None]
    d = {}
    d["tab_words"], d["tab_scales"] = pack_weight(n((K, T)) * s, "e4m3")
    d["offs"] = striped(np.random.permutation(T)[:S])
    d["tab2_words"], d["tab2_scales"] = pack_weight(n((K, T3)) * s, "e4m3")
    d["offs2"] = striped(np.random.permutation(T3)[:P])
    d["pos1"] = striped(np.random.permutation(S)[:P])
    d["w1"] = (1.5 * n((K, H)) / K ** 0.5 / s).astype(np.float32)
    d["ga"] = (np.exp(0.3 * n(H)) * u[:, 0]).astype(np.float32)
    d["gb"] = (0.6 * np.exp(0.3 * n(H)) * u[:, 0]).astype(np.float32)
    d["base"] = (0.7 * n((H, P)) * u).astype(np.float32)
    d["wgs"] = np.exp(0.3 * n((128, P))).astype(np.float32)
    d["w2_words"], d["w2_scales"] = pack_weight(n((H, N)) / H ** 0.5 / u, "e2m1")
    d["w3"] = (n((H, N)) / H ** 0.5 / u).astype(np.float32)
    return d


def reference(tab_words, tab_scales, offs, tab2_words, tab2_scales, offs2, pos1, w1, ga, gb, base, wgs, w2_words, w2_scales, w3):
    v = unpack_weight(tab_words, tab_scales, "e4m3")[:, unstriped(offs)]
    v2 = unpack_weight(tab2_words, tab2_scales, "e4m3")[:, unstriped(offs2)]
    w1q = mxq(f64(w1), 0, "e4m3")
    a = f64(ga)[:, None] * np.tanh(w1q.T @ v)
    b = f64(gb)[:, None] * (w1q.T @ v2) - f64(base)
    placed = np.zeros((H, S))
    placed[:, unstriped(pos1)] = np.tile(f64(wgs), (H // 128, 1)) * b
    z = a - placed
    w2 = unpack_weight(w2_words, w2_scales, "e2m1")
    y = w2.T @ mxq(z, 0, "e4m3")
    y2 = mxq(f64(w3), 0, "e4m3").T @ mxq(placed, 0, "e4m3")
    return np.maximum(y, y2)

@@ -1,0 +1,301 @@
+from contextlib import ExitStack
+
+import concourse.mybir as mybir
+
+F32 = mybir.dt.float32
+BF16 = mybir.dt.bfloat16
+I32 = mybir.dt.int32
+U32 = mybir.dt.uint32
+U16 = mybir.dt.uint16
+U8 = mybir.dt.uint8
+FP8X4 = mybir.dt.float8_e4m3fn_x4
+FP4X4 = mybir.dt.float4_e2m1fn_x4
+ALU = mybir.AluOpType
+ACT = mybir.ActivationFunctionType
+
+K, H, N, T, S, T2, M = 1024, 1024, 384, 4096, 1024, 2048, 512
+P = 128
+PACK = 4
+PASS = P * PACK
+PASSES = 2
+BANK = 512
+CHUNKS = S // BANK
+NSL = N // P
+
+FLOPS = 2 * K * H * (S + M) + 2 * 2 * H * N * S
+
+
+def tile_list_perfusion_viability_scorer_kernel(
+    tc, tab_words, tab_scales, offs, tab2_words, tab2_scales, offs2, pos1, w1, ga, gb, base, wgs, w2_words, w2_scales, w3, out
+):
+    nc = tc.nc
+    with ExitStack() as ctx:
+        keep = ctx.enter_context(tc.tile_pool(name="keep", bufs=1))
+        ring = ctx.enter_context(tc.tile_pool(name="ring", bufs=1))
+        psum = ctx.enter_context(tc.psum_pool(name="psum", bufs=1))
+
+        def held(shape, dtype, name):
+            return keep.tile(shape, dtype, name=name, align_bytes=64)
+
+        def stage(shape, dtype, tag):
+            return ring.tile(shape, dtype, name=tag, tag=tag, align_bytes=64)
+
+        def bank(i):
+            return psum.tile([P, BANK], F32, name="bank%d" % i, tag="bank%d" % i)
+
+        idx = held([P, S // 16], U16, "idx")
+        idx2 = held([P, M // 16], U16, "idx2")
+        place = held([P, M // 16], U16, "place")
+        tab_w = [held([P, T], I32, "tab_w%d" % a) for a in range(PASSES)]
+        tab2_w = [held([P, T2], I32, "tab2_w%d" % a) for a in range(PASSES)]
+        tab_s = held([P, T // 4], I32, "tab_s")
+        tab2_s = held([P, T2 // 4], I32, "tab2_s")
+        v_w = [held([P, S], U32, "v_w%d" % a) for a in range(PASSES)]
+        v2_w = [held([P, M], U32, "v2_w%d" % a) for a in range(PASSES)]
+        v_s = held([P, S], U8, "v_s")
+        v2_s = held([P, M], U8, "v2_s")
+        w1_c = [[held([P, PASS], U32, "w1_c%d%d" % (b, a)) for a in range(PASSES)] for b in range(PASSES)]
+        w1_s = [[held([P, PASS], U8, "w1_s%d%d" % (b, a)) for a in range(PASSES)] for b in range(PASSES)]
+        w3_c = [held([P, N], U32, "w3_c%d" % b) for b in range(PASSES)]
+        w3_s = [held([P, N], U8, "w3_s%d" % b) for b in range(PASSES)]
+        w2_c = held([P, PASSES, 2 * N // 4], I32, "w2_c")
+        w2_s = held([P, PASSES, N // 4], I32, "w2_s")
+        z_c = [[held([P, BANK], U32, "z_c%d%d" % (b, c)) for c in range(CHUNKS)] for b in range(PASSES)]
+        z_s = [[held([P, BANK], U8, "z_s%d%d" % (b, c)) for c in range(CHUNKS)] for b in range(PASSES)]
+        p_c = [[held([P, BANK], U32, "p_c%d%d" % (b, c)) for c in range(CHUNKS)] for b in range(PASSES)]
+        p_s = [[held([P, BANK], U8, "p_s%d%d" % (b, c)) for c in range(CHUNKS)] for b in range(PASSES)]
+        pages = [held([P, S], F32, "page%d" % s) for s in range(PASSES * PACK)]
+        woven = [held([P, BANK * PACK], BF16, "woven%d" % i) for i in range(4)]
+        feats = [held([P, S], F32, "feats%d" % i) for i in range(3)]
+        z_planes = [held([P, PACK, S], BF16, "z_planes%d" % b) for b in range(PASSES)]
+        ga_sb = held([P, PASSES, PACK], F32, "ga_sb")
+        gb_sb = held([P, PASSES, PACK], F32, "gb_sb")
+        wgs_first = held([P, M], F32, "wgs_first")
+        wgs_rest = held([P, PACK - 1, M], F32, "wgs_rest")
+        wgs_t = [wgs_first[:]] + [wgs_rest[:, t, :] for t in range(PACK - 1)]
+
+        def load_scale_rows(queue, tile, src):
+            for q in range(4):
+                queue.dma_start(out=tile[32 * q : 32 * q + 4 * PASSES, :], in_=src[:, 4 * q : 4 * q + 4, :].bitcast(I32))
+
+        def load_words(tile, src, a):
+            nc.sync.dma_start(out=tile[:], in_=src[a].rearrange("p n i -> p (n i)").bitcast(I32))
+
+        def load_w1(b, a):
+            raw = stage([P, PACK, PASS], F32, "wide%d" % (2 * b + a))
+            src = w1[PASS * a : PASS * (a + 1), PASS * b : PASS * (b + 1)]
+            nc.sync.dma_start(out=raw[:], in_=src.rearrange("(p j) c -> p j c", j=PACK))
+            return raw
+
+        def load_base(tile, b, t):
+            src = base[PASS * b : PASS * (b + 1), :].rearrange("(p t) m -> p t m", t=PACK)
+            nc.sync.dma_start(out=tile[:, t, :], in_=src[:, t, :])
+
+        def quantize(codes, scales, src):
+            nc.vector.quantize_mx(out=codes.bitcast(FP8X4), scales=scales, in_=src)
+
+        def quantize_w1(b, a, raw, vector_share):
+            wv = woven[2 * b + a]
+            dst = wv[:].rearrange("p (t m j) -> p m j t", t=PACK, j=PACK)
+            src = raw[:].rearrange("p j (m t) -> p m j t", t=PACK)
+            cut = P - vector_share
+            nc.scalar.copy(out=dst[:, :cut], in_=src[:, :cut])
+            if vector_share:
+                nc.vector.tensor_copy(out=dst[:, cut:], in_=src[:, cut:])
+            quantize(w1_c[b][a][:], w1_s[b][a][:], wv[:])
+
+        def first_product(acc, s, words, scales, cols):
+            b, t = divmod(s, PACK)
+            rows = slice(P * t, P * (t + 1))
+            for a in range(PASSES):
+                nc.tensor.matmul_mx(
+                    out=acc[:],
+                    lhsT=w1_c[b][a][:, rows].bitcast(FP8X4),
+                    lhsT_scale=w1_s[b][a][:, rows],
+                    rhs=words[a][:, cols].bitcast(FP8X4),
+                    rhs_scale=scales[4 * a :, cols],
+                    start=(a == 0),
+                    stop=(a == PASSES - 1),
+                )
+
+        def place_slice(s, reading):
+            b, t = divmod(s, PACK)
+            acc = bank(s % 2)
+            first_product(acc, s, v2_w, v2_s, slice(0, M))
+            nc.vector.scalar_tensor_tensor(
+                out=reading, in0=acc[:], scalar=gb_sb[:, b, t : t + 1], in1=base_sb[b][:, t, :], op0=ALU.mult, op1=ALU.subtract
+            )
+            nc.vector.tensor_tensor(out=pages[s][:].indirect(place[:]), in0=reading, in1=wgs_t[t], op=ALU.mult)
+
+        def feature_slice(s):
+            th = feats[s % 3]
+            for c in range(CHUNKS):
+                cols = slice(BANK * c, BANK * (c + 1))
+                acc = bank(2 + 2 * (s % 3) + c)
+                first_product(acc, s, v_w, v_s, cols)
+                nc.scalar.activation(out=th[:, cols], in_=acc[:], func=ACT.Tanh)
+
+        def difference(s):
+            b, t = divmod(s, PACK)
+            nc.vector.scalar_tensor_tensor(
+                out=z_planes[b][:, t, :],
+                in0=feats[s % 3][:],
+                scalar=ga_sb[:, b, t : t + 1],
+                in1=pages[s][:],
+                op0=ALU.mult,
+                op1=ALU.subtract,
+            )
+
+        def weave(copy, wv, planes, t0):
+            nt = planes.shape[1]
+            dst = wv[:].rearrange("p (c i t) -> p c t i", i=4, t=PACK)[:, :, t0 : t0 + nt, :]
+            copy(out=dst, in_=planes.rearrange("p t (c i) -> p c t i", i=4))
+
+        nc.vector.memset(tab2_s[:], 0)
+        nc.vector.memset(tab_s[:], 0)
+        for page in pages:
+            nc.vector.memset(page[:].bitcast(I32), 0)
+        nc.vector.memset(w2_s[:], 0)
+
+        nc.sync.dma_start(idx2[:], offs2)
+        nc.sync.dma_start(idx[:], offs)
+        nc.sync.dma_start(place[:], pos1)
+        nc.sync.dma_start(out=gb_sb[:], in_=gb.rearrange("(b p t) -> p b t", p=P, t=PACK))
+        w1_raw = {}
+        w1_raw[0, 0] = load_w1(0, 0)
+        w1_raw[0, 1] = load_w1(0, 1)
+        load_scale_rows(nc.scalar, tab2_s, tab2_scales)
+        load_scale_rows(nc.gpsimd, tab_s, tab_scales)
+        load_words(tab2_w[0], tab2_words, 0)
+        load_words(tab2_w[1], tab2_words, 1)
+        base_sb = [stage([P, PACK, M], F32, "base%d" % b) for b in range(PASSES)]
+        wgs_rows = wgs.rearrange("(q t) m -> q t m", t=PACK)
+        load_base(base_sb[0], 0, 0)
+        for g in range(4):
+            nc.sync.dma_start(out=wgs_first[32 * g : 32 * (g + 1), :], in_=wgs_rows[:, 0, :])
+        load_base(base_sb[0], 0, 1)
+        for g in range(4):
+            nc.sync.dma_start(out=wgs_rest[32 * g : 32 * (g + 1)], in_=wgs_rows[:, 1:, :])
+        w1_raw[1, 0] = load_w1(1, 0)
+        w1_raw[1, 1] = load_w1(1, 1)
+        nc.sync.dma_start(out=ga_sb[:], in_=ga.rearrange("(b p t) -> p b t", p=P, t=PACK))
+        load_base(base_sb[0], 0, 2)
+        load_words(tab_w[0], tab_words, 0)
+        w3_raw = []
+        for b in range(PASSES):
+            raw = stage([P, PACK, N], F32, "wide%d" % b)
+            nc.sync.dma_start(out=raw[:], in_=w3[PASS * b : PASS * (b + 1), :].rearrange("(p j) n -> p j n", j=PACK))
+            w3_raw.append(raw)
+        load_words(tab_w[1], tab_words, 1)
+        load_base(base_sb[0], 0, 3)
+        nc.sync.dma_start(out=base_sb[1][:], in_=base[PASS:, :].rearrange("(p t) m -> p t m", t=PACK))
+        nc.sync.dma_start(out=w2_c[:], in_=w2_words.rearrange("a p c -> p a c").bitcast(I32))
+        for q in range(4):
+            nc.sync.dma_start(
+                out=w2_s[32 * q : 32 * q + 4], in_=w2_scales[:, 4 * q : 4 * q + 4, :].rearrange("a r c -> r a c").bitcast(I32)
+            )
+
+        def gather_words(dst, src, offsets):
+            nc.vector.tensor_copy(out=dst[:], in_=src[:].bitcast(U32).indirect(offsets[:]))
+
+        def chunk(c):
+            return slice(BANK * c, BANK * (c + 1))
+
+        quantize_w1(0, 0, w1_raw[0, 0], 0)
+        nc.vector.tensor_copy(out=v2_s[:], in_=tab2_s[:].bitcast(U8).indirect(idx2[:]))
+        quantize_w1(0, 1, w1_raw[0, 1], 64)
+        for a in range(PASSES):
+            gather_words(v2_w[a], tab2_w[a], idx2)
+        nc.vector.tensor_copy(out=v_s[:], in_=tab_s[:].bitcast(U8).indirect(idx[:]))
+
+        for s in range(3):
+            place_slice(s, feats[s][:, :M])
+        for a in range(PASSES):
+            quantize_w1(1, a, w1_raw[1, a], 0)
+        gather_words(v_w[0], tab_w[0], idx)
+        for b in range(PASSES):
+            wv = woven[b]
+            dst = wv[:, : N * PACK].rearrange("p (c i t) -> p c t i", i=4, t=PACK)
+            nc.scalar.copy(out=dst, in_=w3_raw[b][:].rearrange("p t (c i) -> p c t i", i=4))
+            quantize(w3_c[b][:, :256], w3_s[b][:, :256], wv[:, :1024])
+            quantize(w3_c[b][:, 256:], w3_s[b][:, 256:], wv[:, 1024 : N * PACK])
+        gather_words(v_w[1], tab_w[1], idx)
+        place_slice(3, woven[2][:].bitcast(F32)[:, :M])
+
+        p_planes = [stage([P, PACK, BANK], F32, "wide%d" % (2 + c)) for c in range(CHUNKS)]
+        for t in range(PACK):
+            for c in range(CHUNKS):
+                nc.sync.dma_start(out=p_planes[c][:, t, :], in_=pages[t][:, chunk(c)])
+        for s in range(PACK):
+            feature_slice(s)
+            difference(s)
+
+        place_slice(4, feats[0][:, :M])
+        feature_slice(4)
+        difference(4)
+        for c in range(CHUNKS):
+            weave(nc.scalar.copy, woven[2 + c], p_planes[c][:], 0)
+            quantize(p_c[0][c][:], p_s[0][c][:], woven[2 + c][:])
+        place_slice(5, woven[3][:].bitcast(F32)[:, :M])
+        feature_slice(5)
+        difference(5)
+        for c in range(CHUNKS):
+            weave(nc.scalar.copy, woven[c], z_planes[0][:, :, chunk(c)], 0)
+            quantize(z_c[0][c][:], z_s[0][c][:], woven[c][:])
+        place_slice(6, woven[1][:].bitcast(F32)[:, :M])
+        feature_slice(6)
+        difference(6)
+        feature_slice(7)
+        p_wv = woven[:2]
+        z_wv = woven[2:]
+        for c in range(CHUNKS):
+            weave(nc.scalar.copy, z_wv[c], z_planes[1][:, 0:2, chunk(c)], 0)
+        p_three = [stage([P, PACK - 1, BANK], F32, "wide%d" % c) for c in range(CHUNKS)]
+        for t in range(PACK - 1):
+            for c in range(CHUNKS):
+                nc.sync.dma_start(out=p_three[c][:, t, :], in_=pages[PACK + t][:, chunk(c)])
+        place_slice(7, feats[0][:, :M])
+        difference(7)
+        for c in range(CHUNKS):
+            weave(nc.scalar.copy, p_wv[c], p_three[c][:], 0)
+            dst = p_wv[c][:].rearrange("p (j t) -> p j t", t=PACK)[:, :, PACK - 1]
+            nc.scalar.copy(out=dst, in_=pages[7][:, chunk(c)])
+        for c in range(CHUNKS):
+            weave(nc.vector.tensor_copy, z_wv[c], z_planes[1][:, 2:4, chunk(c)], 2)
+        for c in range(CHUNKS):
+            quantize(z_c[1][c][:], z_s[1][c][:], z_wv[c][:])
+        for c in range(CHUNKS):
+            quantize(p_c[1][c][:], p_s[1][c][:], p_wv[c][:])
+
+        w2_codes = w2_c[:].bitcast(U8)
+        w2_scale = w2_s[:].bitcast(U8)
+        y_banks = [[6, 7, 2], [0, 1, 6]]
+        y2_banks = [[3, 4, 5], [7, 2, 3]]
+        for c in range(CHUNKS):
+            res = stage([P, NSL, BANK], F32, "base%d" % c)
+            ys = [bank(i) for i in y_banks[c]]
+            y2s = [bank(i) for i in y2_banks[c]]
+            for b in range(PASSES):
+                for n in range(NSL):
+                    nc.tensor.matmul_mx(
+                        out=ys[n][:],
+                        lhsT=w2_codes[:, b, 2 * P * n : 2 * P * (n + 1)].bitcast(FP4X4),
+                        lhsT_scale=w2_scale[:, b, P * n : P * (n + 1)],
+                        rhs=z_c[b][c][:].bitcast(FP8X4),
+                        rhs_scale=z_s[b][c][:],
+                        start=(b == 0),
+                        stop=(b == PASSES - 1),
+                    )
+                    nc.tensor.matmul_mx(
+                        out=y2s[n][:],
+                        lhsT=w3_c[b][:, P * n : P * (n + 1)].bitcast(FP8X4),
+                        lhsT_scale=w3_s[b][:, P * n : P * (n + 1)],
+                        rhs=p_c[b][c][:].bitcast(FP8X4),
+                        rhs_scale=p_s[b][c][:],
+                        start=(b == 0),
+                        stop=(b == PASSES - 1),
+                    )
+            for n in range(NSL):
+                nc.scalar.copy(out=res[:, n, :], in_=ys[n][:])
+                nc.vector.tensor_tensor(out=res[:, n, :], in0=y2s[n][:], in1=res[:, n, :], op=ALU.max)
+                nc.sync.dma_start(out=out[P * n : P * (n + 1), BANK * c : BANK * (c + 1)], in_=res[:, n, :])

@@ -65,9 +65,8 @@ def tile_list_perfusion_viability_scorer_kernel(
         p_c = [[held([P, BANK], U32, "p_c%d%d" % (b, c)) for c in range(CHUNKS)] for b in range(PASSES)]
         p_s = [[held([P, BANK], U8, "p_s%d%d" % (b, c)) for c in range(CHUNKS)] for b in range(PASSES)]
         pages = [held([P, S], F32, "page%d" % s) for s in range(PASSES * PACK)]
-        woven = [held([P, BANK * PACK], BF16, "woven%d" % i) for i in range(4)]
+        woven = [held([P, BANK * PACK], BF16, "woven%d" % i) for i in range(6)]
         feats = [held([P, S], F32, "feats%d" % i) for i in range(3)]
-        z_planes = [held([P, PACK, S], BF16, "z_planes%d" % b) for b in range(PASSES)]
         ga_sb = held([P, PASSES, PACK], F32, "ga_sb")
         gb_sb = held([P, PASSES, PACK], F32, "gb_sb")
         wgs_first = held([P, M], F32, "wgs_first")
@@ -81,11 +80,9 @@ def tile_list_perfusion_viability_scorer_kernel(
         def load_words(tile, src, a):
             nc.sync.dma_start(out=tile[:], in_=src[a].rearrange("p n i -> p (n i)").bitcast(I32))
 
-        def load_w1(b, a):
-            raw = stage([P, PACK, PASS], F32, "wide%d" % (2 * b + a))
+        def load_w1(b, a, raw):
             src = w1[PASS * a : PASS * (a + 1), PASS * b : PASS * (b + 1)]
-            nc.sync.dma_start(out=raw[:], in_=src.rearrange("(p j) c -> p j c", j=PACK))
-            return raw
+            nc.sync.dma_start(out=raw, in_=src.rearrange("(p j) c -> p j c", j=PACK))
 
         def load_base(tile, b, t):
             src = base[PASS * b : PASS * (b + 1), :].rearrange("(p t) m -> p t m", t=PACK)
@@ -96,8 +93,8 @@ def tile_list_perfusion_viability_scorer_kernel(
 
         def quantize_w1(b, a, raw, vector_share):
             wv = woven[2 * b + a]
-            dst = wv[:].rearrange("p (t m j) -> p m j t", t=PACK, j=PACK)
-            src = raw[:].rearrange("p j (m t) -> p m j t", t=PACK)
+            dst = wv[:].rearrange("p (t m j) -> p m t j", t=PACK, j=PACK)
+            src = raw.rearrange("p j (m t) -> p m t j", t=PACK)
             cut = P - vector_share
             nc.scalar.copy(out=dst[:, :cut], in_=src[:, :cut])
             if vector_share:
@@ -135,13 +132,13 @@ def tile_list_perfusion_viability_scorer_kernel(
                 first_product(acc, s, v_w, v_s, cols)
                 nc.scalar.activation(out=th[:, cols], in_=acc[:], func=ACT.Tanh)
 
-        def difference(s):
+        def difference(s, cols):
             b, t = divmod(s, PACK)
             nc.vector.scalar_tensor_tensor(
-                out=z_planes[b][:, t, :],
-                in0=feats[s % 3][:],
+                out=z_planes[b][:, t, cols],
+                in0=feats[s % 3][:, cols],
                 scalar=ga_sb[:, b, t : t + 1],
-                in1=pages[s][:],
+                in1=pages[s][:, cols],
                 op0=ALU.mult,
                 op1=ALU.subtract,
             )
@@ -153,47 +150,52 @@ def tile_list_perfusion_viability_scorer_kernel(
 
         nc.vector.memset(tab2_s[:], 0)
         nc.vector.memset(tab_s[:], 0)
-        for page in pages:
+        for page in pages[:PACK]:
             nc.vector.memset(page[:].bitcast(I32), 0)
         nc.vector.memset(w2_s[:], 0)
 
+        wgs_rows = wgs.rearrange("(q t) m -> q t m", t=PACK)
         nc.sync.dma_start(idx2[:], offs2)
-        nc.sync.dma_start(idx[:], offs)
-        nc.sync.dma_start(place[:], pos1)
-        nc.sync.dma_start(out=gb_sb[:], in_=gb.rearrange("(b p t) -> p b t", p=P, t=PACK))
-        w1_raw = {}
-        w1_raw[0, 0] = load_w1(0, 0)
-        w1_raw[0, 1] = load_w1(0, 1)
+        for g in range(4):
+            nc.sync.dma_start(out=wgs_first[32 * g : 32 * (g + 1), :], in_=wgs_rows[:, 0, :])
+        w1_first = [stage([P, PACK, PASS], F32, "wide%d" % a) for a in range(PASSES)]
+        for a in range(PASSES):
+            load_w1(0, a, w1_first[a][:])
         load_scale_rows(nc.scalar, tab2_s, tab2_scales)
         load_scale_rows(nc.gpsimd, tab_s, tab_scales)
         load_words(tab2_w[0], tab2_words, 0)
         load_words(tab2_w[1], tab2_words, 1)
+        nc.sync.dma_start(place[:], pos1)
+        nc.sync.dma_start(out=gb_sb[:], in_=gb.rearrange("(b p t) -> p b t", p=P, t=PACK))
         base_sb = [stage([P, PACK, M], F32, "base%d" % b) for b in range(PASSES)]
-        wgs_rows = wgs.rearrange("(q t) m -> q t m", t=PACK)
         load_base(base_sb[0], 0, 0)
-        for g in range(4):
-            nc.sync.dma_start(out=wgs_first[32 * g : 32 * (g + 1), :], in_=wgs_rows[:, 0, :])
+        nc.sync.dma_start(idx[:], offs)
         load_base(base_sb[0], 0, 1)
         for g in range(4):
             nc.sync.dma_start(out=wgs_rest[32 * g : 32 * (g + 1)], in_=wgs_rows[:, 1:, :])
-        w1_raw[1, 0] = load_w1(1, 0)
-        w1_raw[1, 1] = load_w1(1, 1)
-        nc.sync.dma_start(out=ga_sb[:], in_=ga.rearrange("(b p t) -> p b t", p=P, t=PACK))
+        w1_second = stage([P, PASSES, PACK, PASS], F32, "widest")
+        for a in range(PASSES):
+            load_w1(1, a, w1_second[:, a])
         load_base(base_sb[0], 0, 2)
-        load_words(tab_w[0], tab_words, 0)
         w3_raw = []
         for b in range(PASSES):
             raw = stage([P, PACK, N], F32, "wide%d" % b)
             nc.sync.dma_start(out=raw[:], in_=w3[PASS * b : PASS * (b + 1), :].rearrange("(p j) n -> p j n", j=PACK))
             w3_raw.append(raw)
-        load_words(tab_w[1], tab_words, 1)
         load_base(base_sb[0], 0, 3)
-        nc.sync.dma_start(out=base_sb[1][:], in_=base[PASS:, :].rearrange("(p t) m -> p t m", t=PACK))
-        nc.sync.dma_start(out=w2_c[:], in_=w2_words.rearrange("a p c -> p a c").bitcast(I32))
+        load_words(tab_w[0], tab_words, 0)
+        load_words(tab_w[1], tab_words, 1)
+        load_base(base_sb[1], 1, 0)
+        nc.sync.dma_start(out=base_sb[1][:, 1:, :], in_=base[PASS:, :].rearrange("(p t) m -> p t m", t=PACK)[:, 1:, :])
+        nc.gpsimd.dma_start(out=ga_sb[:], in_=ga.rearrange("(b p t) -> p b t", p=P, t=PACK))
+        nc.gpsimd.dma_start(out=w2_c[:], in_=w2_words.rearrange("a p c -> p a c").bitcast(I32))
         for q in range(4):
-            nc.sync.dma_start(
+            nc.gpsimd.dma_start(
                 out=w2_s[32 * q : 32 * q + 4], in_=w2_scales[:, 4 * q : 4 * q + 4, :].rearrange("a r c -> r a c").bitcast(I32)
             )
+
+        for page in pages[PACK:]:
+            nc.gpsimd.memset(page[:].bitcast(I32), 0)
 
         def gather_words(dst, src, offsets):
             nc.vector.tensor_copy(out=dst[:], in_=src[:].bitcast(U32).indirect(offsets[:]))
@@ -201,9 +203,14 @@ def tile_list_perfusion_viability_scorer_kernel(
         def chunk(c):
             return slice(BANK * c, BANK * (c + 1))
 
-        quantize_w1(0, 0, w1_raw[0, 0], 0)
+        def as_reading(wv):
+            return wv[:].bitcast(F32)[:, :M]
+
+        whole = slice(0, S)
+
+        quantize_w1(0, 0, w1_first[0][:], 0)
         nc.vector.tensor_copy(out=v2_s[:], in_=tab2_s[:].bitcast(U8).indirect(idx2[:]))
-        quantize_w1(0, 1, w1_raw[0, 1], 64)
+        quantize_w1(0, 1, w1_first[1][:], 64)
         for a in range(PASSES):
             gather_words(v2_w[a], tab2_w[a], idx2)
         nc.vector.tensor_copy(out=v_s[:], in_=tab_s[:].bitcast(U8).indirect(idx[:]))
@@ -211,61 +218,61 @@ def tile_list_perfusion_viability_scorer_kernel(
         for s in range(3):
             place_slice(s, feats[s][:, :M])
         for a in range(PASSES):
-            quantize_w1(1, a, w1_raw[1, a], 0)
-        gather_words(v_w[0], tab_w[0], idx)
+            quantize_w1(1, a, w1_second[:, a], 0)
+        reading3 = stage([P, M], F32, "widest")
+        place_slice(3, reading3[:])
         for b in range(PASSES):
-            wv = woven[b]
+            wv = woven[4 + b]
             dst = wv[:, : N * PACK].rearrange("p (c i t) -> p c t i", i=4, t=PACK)
             nc.scalar.copy(out=dst, in_=w3_raw[b][:].rearrange("p t (c i) -> p c t i", i=4))
             quantize(w3_c[b][:, :256], w3_s[b][:, :256], wv[:, :1024])
             quantize(w3_c[b][:, 256:], w3_s[b][:, 256:], wv[:, 1024 : N * PACK])
-        gather_words(v_w[1], tab_w[1], idx)
-        place_slice(3, woven[2][:].bitcast(F32)[:, :M])
+        for a in range(PASSES):
+            gather_words(v_w[a], tab_w[a], idx)
+        place_slice(4, as_reading(woven[2]))
 
-        p_planes = [stage([P, PACK, BANK], F32, "wide%d" % (2 + c)) for c in range(CHUNKS)]
+        p_planes = stage([P, PACK, S], F32, "widest")
         for t in range(PACK):
-            for c in range(CHUNKS):
-                nc.sync.dma_start(out=p_planes[c][:, t, :], in_=pages[t][:, chunk(c)])
-        for s in range(PACK):
+            nc.sync.dma_start(out=p_planes[:, t, :], in_=pages[t][:])
+        for c in range(CHUNKS):
+            weave(nc.scalar.copy, woven[c], p_planes[:, :, chunk(c)], 0)
+        z_planes = [stage([P, PACK, S], BF16, "wide1"), stage([P, PACK, S], BF16, "planes")]
+        for s in range(5):
             feature_slice(s)
-            difference(s)
-
-        place_slice(4, feats[0][:, :M])
-        feature_slice(4)
-        difference(4)
-        for c in range(CHUNKS):
-            weave(nc.scalar.copy, woven[2 + c], p_planes[c][:], 0)
-            quantize(p_c[0][c][:], p_s[0][c][:], woven[2 + c][:])
-        place_slice(5, woven[3][:].bitcast(F32)[:, :M])
+            difference(s, whole)
+        place_slice(5, feats[1][:, :M])
         feature_slice(5)
-        difference(5)
+        difference(5, whole)
         for c in range(CHUNKS):
-            weave(nc.scalar.copy, woven[c], z_planes[0][:, :, chunk(c)], 0)
-            quantize(z_c[0][c][:], z_s[0][c][:], woven[c][:])
-        place_slice(6, woven[1][:].bitcast(F32)[:, :M])
+            quantize(p_c[0][c][:], p_s[0][c][:], woven[c][:])
+        place_slice(6, as_reading(woven[1]))
+        for c in range(CHUNKS):
+            weave(nc.scalar.copy, woven[2 + c], z_planes[0][:, :, chunk(c)], 0)
         feature_slice(6)
-        difference(6)
+        difference(6, whole)
         feature_slice(7)
-        p_wv = woven[:2]
-        z_wv = woven[2:]
+        p_pair = stage([P, 2, S], F32, "wide0")
+        for t in range(2):
+            nc.sync.dma_start(out=p_pair[:, t, :], in_=pages[PACK + t][:])
+        p_wv = woven[4:]
+        z_wv = woven[:2]
         for c in range(CHUNKS):
-            weave(nc.scalar.copy, z_wv[c], z_planes[1][:, 0:2, chunk(c)], 0)
-        p_three = [stage([P, PACK - 1, BANK], F32, "wide%d" % c) for c in range(CHUNKS)]
-        for t in range(PACK - 1):
-            for c in range(CHUNKS):
-                nc.sync.dma_start(out=p_three[c][:, t, :], in_=pages[PACK + t][:, chunk(c)])
+            dst = p_wv[c][:].rearrange("p (j t) -> p j t", t=PACK)[:, :, 0:2]
+            nc.scalar.copy(out=dst, in_=p_pair[:, :, chunk(c)].rearrange("p t j -> p j t"))
         place_slice(7, feats[0][:, :M])
-        difference(7)
+        for t in range(2, PACK):
+            for c in range(CHUNKS):
+                dst = p_wv[c][:].rearrange("p (j t) -> p j t", t=PACK)[:, :, t]
+                nc.scalar.copy(out=dst, in_=pages[PACK + t][:, chunk(c)])
         for c in range(CHUNKS):
-            weave(nc.scalar.copy, p_wv[c], p_three[c][:], 0)
-            dst = p_wv[c][:].rearrange("p (j t) -> p j t", t=PACK)[:, :, PACK - 1]
-            nc.scalar.copy(out=dst, in_=pages[7][:, chunk(c)])
+            difference(7, chunk(c))
         for c in range(CHUNKS):
-            weave(nc.vector.tensor_copy, z_wv[c], z_planes[1][:, 2:4, chunk(c)], 2)
-        for c in range(CHUNKS):
-            quantize(z_c[1][c][:], z_s[1][c][:], z_wv[c][:])
+            quantize(z_c[0][c][:], z_s[0][c][:], woven[2 + c][:])
+        weave(nc.vector.tensor_copy, z_wv[0], z_planes[1][:, :, chunk(0)], 0)
+        weave(nc.scalar.copy, z_wv[1], z_planes[1][:, :, chunk(1)], 0)
         for c in range(CHUNKS):
             quantize(p_c[1][c][:], p_s[1][c][:], p_wv[c][:])
+            quantize(z_c[1][c][:], z_s[1][c][:], z_wv[c][:])
 
         w2_codes = w2_c[:].bitcast(U8)
         w2_scale = w2_s[:].bitcast(U8)

@@ -13,14 +13,25 @@ FP4X4 = mybir.dt.float4_e2m1fn_x4
 ALU = mybir.AluOpType
 ACT = mybir.ActivationFunctionType
 
-K, H, N, T, S, T2, M = 1024, 1024, 384, 4096, 1024, 2048, 512
+K, H, N = 1024, 1024, 384
+T, S = 4096, 1024
+T2, M = 2048, 512
+
 P = 128
 PACK = 4
 PASS = P * PACK
 PASSES = 2
+SLICES = PASSES * PACK
+QUADRANTS = 4
+QUAD = P // QUADRANTS
+SCALE_ROWS = 4
 BANK = 512
 CHUNKS = S // BANK
-NSL = N // P
+WOVEN = BANK * PACK
+OUT_SLICES = N // P
+RUN = 4
+FEATS = 5
+WIDE_QUANTIZE = 2048
 
 FLOPS = 2 * K * H * (S + M) + 2 * 2 * H * N * S
 
@@ -31,278 +42,288 @@ def tile_list_perfusion_viability_scorer_kernel(
     nc = tc.nc
     with ExitStack() as ctx:
         keep = ctx.enter_context(tc.tile_pool(name="keep", bufs=1))
-        ring = ctx.enter_context(tc.tile_pool(name="ring", bufs=1))
+        shared = ctx.enter_context(tc.tile_pool(name="shared", bufs=1))
         psum = ctx.enter_context(tc.psum_pool(name="psum", bufs=1))
 
         def held(shape, dtype, name):
             return keep.tile(shape, dtype, name=name, align_bytes=64)
 
-        def stage(shape, dtype, tag):
-            return ring.tile(shape, dtype, name=tag, tag=tag, align_bytes=64)
+        def tenant(shape, dtype, tag):
+            return shared.tile(shape, dtype, name=tag, tag=tag, align_bytes=64)
 
         def bank(i):
             return psum.tile([P, BANK], F32, name="bank%d" % i, tag="bank%d" % i)
 
+        def chunk(c):
+            return slice(BANK * c, BANK * (c + 1))
+
         idx = held([P, S // 16], U16, "idx")
         idx2 = held([P, M // 16], U16, "idx2")
         place = held([P, M // 16], U16, "place")
-        tab_w = [held([P, T], I32, "tab_w%d" % a) for a in range(PASSES)]
-        tab2_w = [held([P, T2], I32, "tab2_w%d" % a) for a in range(PASSES)]
+        tab_w = [tenant([P, T], I32, "tab_w%d" % g) for g in range(PASSES)]
+        tab2_w = [held([P, T2], I32, "tab2_w%d" % g) for g in range(PASSES)]
         tab_s = held([P, T // 4], I32, "tab_s")
         tab2_s = held([P, T2 // 4], I32, "tab2_s")
-        v_w = [held([P, S], U32, "v_w%d" % a) for a in range(PASSES)]
-        v2_w = [held([P, M], U32, "v2_w%d" % a) for a in range(PASSES)]
+        v_w = [held([P, S], U32, "v_w%d" % g) for g in range(PASSES)]
+        v2_w = [held([P, M], U32, "v2_w%d" % g) for g in range(PASSES)]
         v_s = held([P, S], U8, "v_s")
         v2_s = held([P, M], U8, "v2_s")
-        w1_c = [[held([P, PASS], U32, "w1_c%d%d" % (b, a)) for a in range(PASSES)] for b in range(PASSES)]
-        w1_s = [[held([P, PASS], U8, "w1_s%d%d" % (b, a)) for a in range(PASSES)] for b in range(PASSES)]
-        w3_c = [held([P, N], U32, "w3_c%d" % b) for b in range(PASSES)]
-        w3_s = [held([P, N], U8, "w3_s%d" % b) for b in range(PASSES)]
+        w1_c = [held([P, PASSES * PASS], U32, "w1_c")]
+        w1_s = [held([P, PASSES * PASS], U8, "w1_s%d" % h) for h in range(PASSES)]
         w2_c = held([P, PASSES, 2 * N // 4], I32, "w2_c")
         w2_s = held([P, PASSES, N // 4], I32, "w2_s")
-        z_c = [[held([P, BANK], U32, "z_c%d%d" % (b, c)) for c in range(CHUNKS)] for b in range(PASSES)]
-        z_s = [[held([P, BANK], U8, "z_s%d%d" % (b, c)) for c in range(CHUNKS)] for b in range(PASSES)]
-        p_c = [[held([P, BANK], U32, "p_c%d%d" % (b, c)) for c in range(CHUNKS)] for b in range(PASSES)]
-        p_s = [[held([P, BANK], U8, "p_s%d%d" % (b, c)) for c in range(CHUNKS)] for b in range(PASSES)]
-        pages = [held([P, S], F32, "page%d" % s) for s in range(PASSES * PACK)]
-        woven = [held([P, BANK * PACK], BF16, "woven%d" % i) for i in range(6)]
-        feats = [held([P, S], F32, "feats%d" % i) for i in range(3)]
+        w3_s = held([P, PASSES * N], U8, "w3_s")
+        placed0_s = held([P, S], U8, "placed0_s")
+        z0_c = held([P, S], U32, "z0_c")
+        z0_s = held([P, S], U8, "z0_s")
+        last_c = [held([P, 2 * BANK], U32, "last_c%d" % c) for c in range(CHUNKS)]
+        last_s = [held([P, 2 * BANK], U8, "last_s%d" % c) for c in range(CHUNKS)]
+        pages = [held([P, S], F32, "page%d" % s) for s in range(SLICES)]
+        woven = [held([P, 2 * WOVEN], BF16, "woven%d" % i) for i in range(3)]
+        feats = [held([P, S], F32, "feats%d" % i) for i in range(FEATS)]
         ga_sb = held([P, PASSES, PACK], F32, "ga_sb")
         gb_sb = held([P, PASSES, PACK], F32, "gb_sb")
-        wgs_first = held([P, M], F32, "wgs_first")
-        wgs_rest = held([P, PACK - 1, M], F32, "wgs_rest")
-        wgs_t = [wgs_first[:]] + [wgs_rest[:, t, :] for t in range(PACK - 1)]
+        wgs_early = [held([P, M], F32, "wgs_early%d" % t) for t in range(2)]
+        wgs_late = held([P, 2, M], F32, "wgs_late")
+        wgs_plane = [wgs_early[0][:], wgs_early[1][:], wgs_late[:, 0, :], wgs_late[:, 1, :]]
+
+        def half(tile, i):
+            return tile[:, WOVEN * i : WOVEN * (i + 1)]
+
+        def quadrant(q, rows):
+            return slice(QUAD * q, QUAD * q + rows)
 
         def load_scale_rows(queue, tile, src):
-            for q in range(4):
-                queue.dma_start(out=tile[32 * q : 32 * q + 4 * PASSES, :], in_=src[:, 4 * q : 4 * q + 4, :].bitcast(I32))
+            for q in range(QUADRANTS):
+                rows = src[:, SCALE_ROWS * q : SCALE_ROWS * (q + 1), :]
+                queue.dma_start(out=tile[quadrant(q, SCALE_ROWS * PASSES), :], in_=rows.bitcast(I32))
 
-        def load_words(tile, src, a):
-            nc.sync.dma_start(out=tile[:], in_=src[a].rearrange("p n i -> p (n i)").bitcast(I32))
+        def load_words(tile, src, g):
+            nc.sync.dma_start(out=tile[:], in_=src[g].rearrange("p n i -> p (n i)").bitcast(I32))
 
-        def load_w1(b, a, raw):
-            src = w1[PASS * a : PASS * (a + 1), PASS * b : PASS * (b + 1)]
-            nc.sync.dma_start(out=raw, in_=src.rearrange("(p j) c -> p j c", j=PACK))
+        def load_rows(tile, src, g):
+            nc.sync.dma_start(out=tile[:], in_=src[PASS * g : PASS * (g + 1), :].rearrange("(p t) c -> p t c", t=PACK))
 
-        def load_base(tile, b, t):
-            src = base[PASS * b : PASS * (b + 1), :].rearrange("(p t) m -> p t m", t=PACK)
-            nc.sync.dma_start(out=tile[:, t, :], in_=src[:, t, :])
+        def load_base(g, planes):
+            src = base[PASS * g : PASS * (g + 1), :].rearrange("(p t) m -> p t m", t=PACK)
+            nc.sync.dma_start(out=base_sb[g][:, planes, :], in_=src[:, planes, :])
+
+        def gather(dst, window, dtype, offsets):
+            nc.vector.tensor_copy(out=dst[:], in_=window[:].bitcast(dtype).indirect(offsets[:]))
 
         def quantize(codes, scales, src):
             nc.vector.quantize_mx(out=codes.bitcast(FP8X4), scales=scales, in_=src)
 
-        def quantize_w1(b, a, raw, vector_share):
-            wv = woven[2 * b + a]
-            dst = wv[:].rearrange("p (t m j) -> p m t j", t=PACK, j=PACK)
-            src = raw.rearrange("p j (m t) -> p m t j", t=PACK)
-            cut = P - vector_share
-            nc.scalar.copy(out=dst[:, :cut], in_=src[:, :cut])
-            if vector_share:
-                nc.vector.tensor_copy(out=dst[:, cut:], in_=src[:, cut:])
-            quantize(w1_c[b][a][:], w1_s[b][a][:], wv[:])
+        def weave(copy, dst, planes):
+            copy(
+                out=dst.rearrange("p (c i t) -> p c t i", i=RUN, t=PACK),
+                in_=planes.rearrange("p t (c i) -> p c t i", i=RUN),
+            )
+
+        def weave_w1(copy, dst, raw, cols):
+            copy(
+                out=dst.rearrange("p (t m j) -> p m t j", t=PACK, j=PACK)[:, cols],
+                in_=raw[:].rearrange("p j (m t) -> p m t j", t=PACK)[:, cols],
+            )
+
+        def weave_page(s, dst):
+            for c in range(CHUNKS):
+                nc.scalar.copy(out=dst[c].rearrange("p (j t) -> p j t", t=PACK)[:, :, s % PACK], in_=pages[s][:, chunk(c)])
 
         def first_product(acc, s, words, scales, cols):
-            b, t = divmod(s, PACK)
-            rows = slice(P * t, P * (t + 1))
-            for a in range(PASSES):
+            h, t = divmod(s, PACK)
+            for g in range(PASSES):
+                rows = slice(PASS * g + P * t, PASS * g + P * (t + 1))
                 nc.tensor.matmul_mx(
                     out=acc[:],
-                    lhsT=w1_c[b][a][:, rows].bitcast(FP8X4),
-                    lhsT_scale=w1_s[b][a][:, rows],
-                    rhs=words[a][:, cols].bitcast(FP8X4),
-                    rhs_scale=scales[4 * a :, cols],
-                    start=(a == 0),
-                    stop=(a == PASSES - 1),
+                    lhsT=w1_c[h][:, rows].bitcast(FP8X4),
+                    lhsT_scale=w1_s[h][:, rows],
+                    rhs=words[g][:, cols].bitcast(FP8X4),
+                    rhs_scale=scales[SCALE_ROWS * g :, cols],
+                    start=(g == 0),
+                    stop=(g == PASSES - 1),
                 )
 
-        def place_slice(s, reading):
-            b, t = divmod(s, PACK)
+        def place_slice(s, b_sb):
+            h, t = divmod(s, PACK)
             acc = bank(s % 2)
             first_product(acc, s, v2_w, v2_s, slice(0, M))
             nc.vector.scalar_tensor_tensor(
-                out=reading, in0=acc[:], scalar=gb_sb[:, b, t : t + 1], in1=base_sb[b][:, t, :], op0=ALU.mult, op1=ALU.subtract
+                out=b_sb, in0=acc[:], scalar=gb_sb[:, h, t : t + 1], in1=base_sb[h][:, t, :], op0=ALU.mult, op1=ALU.subtract
             )
-            nc.vector.tensor_tensor(out=pages[s][:].indirect(place[:]), in0=reading, in1=wgs_t[t], op=ALU.mult)
+            nc.vector.tensor_tensor(out=pages[s][:].indirect(place[:]), in0=b_sb, in1=wgs_plane[t], op=ALU.mult)
 
         def feature_slice(s):
-            th = feats[s % 3]
             for c in range(CHUNKS):
-                cols = slice(BANK * c, BANK * (c + 1))
-                acc = bank(2 + 2 * (s % 3) + c)
-                first_product(acc, s, v_w, v_s, cols)
-                nc.scalar.activation(out=th[:, cols], in_=acc[:], func=ACT.Tanh)
+                acc = bank(2 + CHUNKS * (s % 3) + c)
+                first_product(acc, s, v_w, v_s, chunk(c))
+                nc.scalar.activation(out=feats[s % FEATS][:, chunk(c)], in_=acc[:], func=ACT.Tanh)
 
         def difference(s, cols):
-            b, t = divmod(s, PACK)
+            h, t = divmod(s, PACK)
             nc.vector.scalar_tensor_tensor(
-                out=z_planes[b][:, t, cols],
-                in0=feats[s % 3][:, cols],
-                scalar=ga_sb[:, b, t : t + 1],
+                out=z_planes[h][:, t, cols],
+                in0=feats[s % FEATS][:, cols],
+                scalar=ga_sb[:, h, t : t + 1],
                 in1=pages[s][:, cols],
                 op0=ALU.mult,
                 op1=ALU.subtract,
             )
 
-        def weave(copy, wv, planes, t0):
-            nt = planes.shape[1]
-            dst = wv[:].rearrange("p (c i t) -> p c t i", i=4, t=PACK)[:, :, t0 : t0 + nt, :]
-            copy(out=dst, in_=planes.rearrange("p t (c i) -> p c t i", i=4))
-
         nc.vector.memset(tab2_s[:], 0)
-        nc.vector.memset(tab_s[:], 0)
+        nc.gpsimd.memset(tab_s[:], 0)
         for page in pages[:PACK]:
             nc.vector.memset(page[:].bitcast(I32), 0)
         nc.vector.memset(w2_s[:], 0)
 
         wgs_rows = wgs.rearrange("(q t) m -> q t m", t=PACK)
         nc.sync.dma_start(idx2[:], offs2)
-        for g in range(4):
-            nc.sync.dma_start(out=wgs_first[32 * g : 32 * (g + 1), :], in_=wgs_rows[:, 0, :])
-        w1_first = [stage([P, PACK, PASS], F32, "wide%d" % a) for a in range(PASSES)]
-        for a in range(PASSES):
-            load_w1(0, a, w1_first[a][:])
+        nc.sync.dma_start(place[:], pos1)
+        nc.sync.dma_start(out=gb_sb[:], in_=gb.rearrange("(h p t) -> p h t", p=P, t=PACK))
+        w1_raw = [[tenant([P, PACK, PASS], F32, "wide%d" % (PASSES * h + g)) for g in range(PASSES)] for h in range(PASSES)]
+        for g in range(PASSES):
+            load_rows(w1_raw[0][g], w1[:, :PASS], g)
         load_scale_rows(nc.scalar, tab2_s, tab2_scales)
         load_scale_rows(nc.gpsimd, tab_s, tab_scales)
-        load_words(tab2_w[0], tab2_words, 0)
-        load_words(tab2_w[1], tab2_words, 1)
-        nc.sync.dma_start(place[:], pos1)
-        nc.sync.dma_start(out=gb_sb[:], in_=gb.rearrange("(b p t) -> p b t", p=P, t=PACK))
-        base_sb = [stage([P, PACK, M], F32, "base%d" % b) for b in range(PASSES)]
-        load_base(base_sb[0], 0, 0)
-        nc.sync.dma_start(idx[:], offs)
-        load_base(base_sb[0], 0, 1)
-        for g in range(4):
-            nc.sync.dma_start(out=wgs_rest[32 * g : 32 * (g + 1)], in_=wgs_rows[:, 1:, :])
-        w1_second = stage([P, PASSES, PACK, PASS], F32, "widest")
-        for a in range(PASSES):
-            load_w1(1, a, w1_second[:, a])
-        load_base(base_sb[0], 0, 2)
-        w3_raw = []
-        for b in range(PASSES):
-            raw = stage([P, PACK, N], F32, "wide%d" % b)
-            nc.sync.dma_start(out=raw[:], in_=w3[PASS * b : PASS * (b + 1), :].rearrange("(p j) n -> p j n", j=PACK))
-            w3_raw.append(raw)
-        load_base(base_sb[0], 0, 3)
-        load_words(tab_w[0], tab_words, 0)
-        load_words(tab_w[1], tab_words, 1)
-        load_base(base_sb[1], 1, 0)
-        nc.sync.dma_start(out=base_sb[1][:, 1:, :], in_=base[PASS:, :].rearrange("(p t) m -> p t m", t=PACK)[:, 1:, :])
-        nc.gpsimd.dma_start(out=ga_sb[:], in_=ga.rearrange("(b p t) -> p b t", p=P, t=PACK))
-        nc.gpsimd.dma_start(out=w2_c[:], in_=w2_words.rearrange("a p c -> p a c").bitcast(I32))
-        for q in range(4):
-            nc.gpsimd.dma_start(
-                out=w2_s[32 * q : 32 * q + 4], in_=w2_scales[:, 4 * q : 4 * q + 4, :].rearrange("a r c -> r a c").bitcast(I32)
-            )
+        for g in range(PASSES):
+            load_words(tab2_w[g], tab2_words, g)
+        base_sb = [tenant([P, PACK, M], F32, "base%d" % g) for g in range(PASSES)]
 
+        def load_plane_operands(t):
+            load_base(0, t)
+            for q in range(QUADRANTS):
+                nc.sync.dma_start(out=wgs_early[t][quadrant(q, QUAD), :], in_=wgs_rows[:, t, :])
+
+        load_plane_operands(0)
+        nc.sync.dma_start(idx[:], offs)
+        load_rows(w1_raw[1][0], w1[:, PASS:], 0)
+        load_plane_operands(1)
+        load_rows(w1_raw[1][1], w1[:, PASS:], 1)
+        load_base(0, 2)
+        for q in range(QUADRANTS):
+            nc.sync.dma_start(out=wgs_late[quadrant(q, QUAD)], in_=wgs_rows[:, 2:, :])
+        load_base(0, 3)
+        w3_raw = [tenant([P, PACK, N], F32, "wide%d" % g) for g in range(PASSES)]
+        for g in range(PASSES):
+            load_rows(w3_raw[g], w3, g)
+        for g in range(PASSES):
+            load_words(tab_w[g], tab_words, g)
+        load_base(1, 0)
+        nc.sync.dma_start(out=ga_sb[:], in_=ga.rearrange("(h p t) -> p h t", p=P, t=PACK))
+        load_base(1, slice(1, PACK))
+        for q in range(QUADRANTS):
+            rows = w2_scales[:, SCALE_ROWS * q : SCALE_ROWS * (q + 1), :].rearrange("g r c -> r g c")
+            nc.gpsimd.dma_start(out=w2_s[quadrant(q, SCALE_ROWS)], in_=rows.bitcast(I32))
+        nc.sync.dma_start(out=w2_c[:], in_=w2_words.rearrange("g p c -> p g c").bitcast(I32))
         for page in pages[PACK:]:
             nc.gpsimd.memset(page[:].bitcast(I32), 0)
 
-        def gather_words(dst, src, offsets):
-            nc.vector.tensor_copy(out=dst[:], in_=src[:].bitcast(U32).indirect(offsets[:]))
+        weave_w1(nc.scalar.copy, half(woven[0], 0), w1_raw[0][0], slice(0, P))
+        quantize(w1_c[0][:, :PASS], w1_s[0][:, :PASS], half(woven[0], 0))
+        gather(v2_s, tab2_s, U8, idx2)
+        weave_w1(nc.scalar.copy, half(woven[0], 1), w1_raw[0][1], slice(0, P // 2))
+        weave_w1(nc.vector.tensor_copy, half(woven[0], 1), w1_raw[0][1], slice(P // 2, P))
+        quantize(w1_c[0][:, PASS:], w1_s[0][:, PASS:], half(woven[0], 1))
+        for g in range(PASSES):
+            gather(v2_w[g], tab2_w[g], U32, idx2)
+        gather(v_s, tab_s, U8, idx)
 
-        def chunk(c):
-            return slice(BANK * c, BANK * (c + 1))
-
-        def as_reading(wv):
-            return wv[:].bitcast(F32)[:, :M]
-
-        whole = slice(0, S)
-
-        quantize_w1(0, 0, w1_first[0][:], 0)
-        nc.vector.tensor_copy(out=v2_s[:], in_=tab2_s[:].bitcast(U8).indirect(idx2[:]))
-        quantize_w1(0, 1, w1_first[1][:], 64)
-        for a in range(PASSES):
-            gather_words(v2_w[a], tab2_w[a], idx2)
-        nc.vector.tensor_copy(out=v_s[:], in_=tab_s[:].bitcast(U8).indirect(idx[:]))
-
-        for s in range(3):
+        placed0_woven = [half(woven[0], c) for c in range(CHUNKS)]
+        for s in range(2):
             place_slice(s, feats[s][:, :M])
-        for a in range(PASSES):
-            quantize_w1(1, a, w1_second[:, a], 0)
-        reading3 = stage([P, M], F32, "widest")
-        place_slice(3, reading3[:])
-        for b in range(PASSES):
-            wv = woven[4 + b]
-            dst = wv[:, : N * PACK].rearrange("p (c i t) -> p c t i", i=4, t=PACK)
-            nc.scalar.copy(out=dst, in_=w3_raw[b][:].rearrange("p t (c i) -> p c t i", i=4))
-            quantize(w3_c[b][:, :256], w3_s[b][:, :256], wv[:, :1024])
-            quantize(w3_c[b][:, 256:], w3_s[b][:, 256:], wv[:, 1024 : N * PACK])
-        for a in range(PASSES):
-            gather_words(v_w[a], tab_w[a], idx)
-        place_slice(4, as_reading(woven[2]))
+            weave_page(s, placed0_woven)
+            weave_w1(nc.scalar.copy, half(woven[1], s), w1_raw[1][s], slice(0, P))
+        for g in range(PASSES):
+            weave(nc.scalar.copy, woven[2][:, N * PACK * g : N * PACK * (g + 1)], w3_raw[g][:])
+        for s in range(2, PACK):
+            place_slice(s, feats[s][:, :M])
+            weave_page(s, placed0_woven)
 
-        p_planes = stage([P, PACK, S], F32, "widest")
-        for t in range(PACK):
-            nc.sync.dma_start(out=p_planes[:, t, :], in_=pages[t][:])
-        for c in range(CHUNKS):
-            weave(nc.scalar.copy, woven[c], p_planes[:, :, chunk(c)], 0)
-        z_planes = [stage([P, PACK, S], BF16, "wide1"), stage([P, PACK, S], BF16, "planes")]
-        for s in range(5):
+        gather(v_w[0], tab_w[0], U32, idx)
+        w1_c.append(tenant([P, PASSES * PASS], U32, "tab_w0"))
+        quantize(w1_c[1][:], w1_s[1][:], woven[1][:])
+        gather(v_w[1], tab_w[1], U32, idx)
+
+        b4_sb = tenant([P, M], F32, "late")
+        place_slice(PACK, b4_sb[:])
+        late_c = tenant([P, S + PASSES * N], U32, "late")
+        placed0_c = late_c[:, :S]
+        w3_c = late_c[:, S:]
+        quantize(placed0_c, placed0_s[:], woven[0][:])
+        cut = WIDE_QUANTIZE // PACK
+        quantize(w3_c[:, :cut], w3_s[:, :cut], woven[2][:, :WIDE_QUANTIZE])
+        quantize(w3_c[:, cut:], w3_s[:, cut:], woven[2][:, WIDE_QUANTIZE : PASSES * N * PACK])
+
+        z_planes = [tenant([P, PACK, S], BF16, "wide%d" % (PASSES + g)) for g in range(PASSES)]
+        for s in range(PACK):
             feature_slice(s)
-            difference(s, whole)
-        place_slice(5, feats[1][:, :M])
-        feature_slice(5)
-        difference(5, whole)
+            difference(s, slice(0, S))
+        feature_slice(PACK)
+        for s in range(PACK + 1, SLICES):
+            place_slice(s, feats[(s - 2) % FEATS][:, :M])
+            difference(s - 1, slice(0, S))
+            feature_slice(s)
         for c in range(CHUNKS):
-            quantize(p_c[0][c][:], p_s[0][c][:], woven[c][:])
-        place_slice(6, as_reading(woven[1]))
-        for c in range(CHUNKS):
-            weave(nc.scalar.copy, woven[2 + c], z_planes[0][:, :, chunk(c)], 0)
-        feature_slice(6)
-        difference(6, whole)
-        feature_slice(7)
-        p_pair = stage([P, 2, S], F32, "wide0")
+            weave(nc.scalar.copy, half(woven[1], c), z_planes[0][:, :, chunk(c)])
+
+        last_woven = [woven[2], woven[0]]
+        placed1_woven = [half(last_woven[c], 0) for c in range(CHUNKS)]
+        pair = tenant([P, 2, S], F32, "base0")
         for t in range(2):
-            nc.sync.dma_start(out=p_pair[:, t, :], in_=pages[PACK + t][:])
-        p_wv = woven[4:]
-        z_wv = woven[:2]
+            nc.sync.dma_start(out=pair[:, t, :], in_=pages[PACK + t][:])
         for c in range(CHUNKS):
-            dst = p_wv[c][:].rearrange("p (j t) -> p j t", t=PACK)[:, :, 0:2]
-            nc.scalar.copy(out=dst, in_=p_pair[:, :, chunk(c)].rearrange("p t j -> p j t"))
-        place_slice(7, feats[0][:, :M])
-        for t in range(2, PACK):
-            for c in range(CHUNKS):
-                dst = p_wv[c][:].rearrange("p (j t) -> p j t", t=PACK)[:, :, t]
-                nc.scalar.copy(out=dst, in_=pages[PACK + t][:, chunk(c)])
+            nc.scalar.copy(
+                out=placed1_woven[c].rearrange("p (j t) -> p j t", t=PACK)[:, :, 0:2],
+                in_=pair[:, :, chunk(c)].rearrange("p t j -> p j t"),
+            )
+        for s in range(PACK + 2, SLICES):
+            weave_page(s, placed1_woven)
         for c in range(CHUNKS):
-            difference(7, chunk(c))
+            difference(SLICES - 1, chunk(c))
         for c in range(CHUNKS):
-            quantize(z_c[0][c][:], z_s[0][c][:], woven[2 + c][:])
-        weave(nc.vector.tensor_copy, z_wv[0], z_planes[1][:, :, chunk(0)], 0)
-        weave(nc.scalar.copy, z_wv[1], z_planes[1][:, :, chunk(1)], 0)
+            quantize(z0_c[:, chunk(c)], z0_s[:, chunk(c)], half(woven[1], c))
+        quarter = BANK // 2
+        z1_woven = [half(last_woven[c], 1) for c in range(CHUNKS)]
+        weave(nc.vector.tensor_copy, z1_woven[0], z_planes[1][:, :, chunk(0)])
+        weave(nc.scalar.copy, z1_woven[1][:, : quarter * PACK], z_planes[1][:, :, BANK : BANK + quarter])
         for c in range(CHUNKS):
-            quantize(p_c[1][c][:], p_s[1][c][:], p_wv[c][:])
-            quantize(z_c[1][c][:], z_s[1][c][:], z_wv[c][:])
+            quantize(last_c[c][:, :BANK], last_s[c][:, :BANK], placed1_woven[c])
+        quantize(last_c[0][:, BANK:], last_s[0][:, BANK:], z1_woven[0])
+        weave(nc.vector.tensor_copy, z1_woven[1][:, quarter * PACK :], z_planes[1][:, :, BANK + quarter :])
+        quantize(last_c[1][:, BANK:], last_s[1][:, BANK:], z1_woven[1])
 
         w2_codes = w2_c[:].bitcast(U8)
         w2_scale = w2_s[:].bitcast(U8)
         y_banks = [[6, 7, 2], [0, 1, 6]]
         y2_banks = [[3, 4, 5], [7, 2, 3]]
         for c in range(CHUNKS):
-            res = stage([P, NSL, BANK], F32, "base%d" % c)
-            ys = [bank(i) for i in y_banks[c]]
-            y2s = [bank(i) for i in y2_banks[c]]
-            for b in range(PASSES):
-                for n in range(NSL):
+            z_ops = [(z0_c[:, chunk(c)], z0_s[:, chunk(c)]), (last_c[c][:, BANK:], last_s[c][:, BANK:])]
+            placed_ops = [(placed0_c[:, chunk(c)], placed0_s[:, chunk(c)]), (last_c[c][:, :BANK], last_s[c][:, :BANK])]
+            res = tenant([P, OUT_SLICES, BANK], F32, "base%d" % c)
+            y = [bank(i) for i in y_banks[c]]
+            y2 = [bank(i) for i in y2_banks[c]]
+            for g in range(PASSES):
+                for n in range(OUT_SLICES):
+                    w3_cols = slice(N * g + P * n, N * g + P * (n + 1))
                     nc.tensor.matmul_mx(
-                        out=ys[n][:],
-                        lhsT=w2_codes[:, b, 2 * P * n : 2 * P * (n + 1)].bitcast(FP4X4),
-                        lhsT_scale=w2_scale[:, b, P * n : P * (n + 1)],
-                        rhs=z_c[b][c][:].bitcast(FP8X4),
-                        rhs_scale=z_s[b][c][:],
-                        start=(b == 0),
-                        stop=(b == PASSES - 1),
+                        out=y[n][:],
+                        lhsT=w2_codes[:, g, 2 * P * n : 2 * P * (n + 1)].bitcast(FP4X4),
+                        lhsT_scale=w2_scale[:, g, P * n : P * (n + 1)],
+                        rhs=z_ops[g][0].bitcast(FP8X4),
+                        rhs_scale=z_ops[g][1],
+                        start=(g == 0),
+                        stop=(g == PASSES - 1),
                     )
                     nc.tensor.matmul_mx(
-                        out=y2s[n][:],
-                        lhsT=w3_c[b][:, P * n : P * (n + 1)].bitcast(FP8X4),
-                        lhsT_scale=w3_s[b][:, P * n : P * (n + 1)],
-                        rhs=p_c[b][c][:].bitcast(FP8X4),
-                        rhs_scale=p_s[b][c][:],
-                        start=(b == 0),
-                        stop=(b == PASSES - 1),
+                        out=y2[n][:],
+                        lhsT=w3_c[:, w3_cols].bitcast(FP8X4),
+                        lhsT_scale=w3_s[:, w3_cols],
+                        rhs=placed_ops[g][0].bitcast(FP8X4),
+                        rhs_scale=placed_ops[g][1],
+                        start=(g == 0),
+                        stop=(g == PASSES - 1),
                     )
-            for n in range(NSL):
-                nc.scalar.copy(out=res[:, n, :], in_=ys[n][:])
-                nc.vector.tensor_tensor(out=res[:, n, :], in0=y2s[n][:], in1=res[:, n, :], op=ALU.max)
-                nc.sync.dma_start(out=out[P * n : P * (n + 1), BANK * c : BANK * (c + 1)], in_=res[:, n, :])
+            for n in range(OUT_SLICES):
+                nc.scalar.copy(out=res[:, n, :], in_=y[n][:])
+                nc.vector.tensor_tensor(out=res[:, n, :], in0=y2[n][:], in1=res[:, n, :], op=ALU.max)
+                nc.sync.dma_start(out=out[P * n : P * (n + 1), chunk(c)], in_=res[:, n, :])

from contextlib import ExitStack

import concourse.mybir as mybir

F32 = mybir.dt.float32
BF16 = mybir.dt.bfloat16
I32 = mybir.dt.int32
U32 = mybir.dt.uint32
U16 = mybir.dt.uint16
U8 = mybir.dt.uint8
FP8X4 = mybir.dt.float8_e4m3fn_x4
FP4X4 = mybir.dt.float4_e2m1fn_x4
ALU = mybir.AluOpType
ACT = mybir.ActivationFunctionType

K, H, N = 1024, 1024, 384
T, S = 4096, 1024
T2, M = 2048, 512

P = 128
PACK = 4
PASS = P * PACK
PASSES = 2
SLICES = PASSES * PACK
QUADRANTS = 4
QUAD = P // QUADRANTS
SCALE_ROWS = 4
BANK = 512
CHUNKS = S // BANK
WOVEN = BANK * PACK
OUT_SLICES = N // P
RUN = 4
FEATS = 5
WIDE_QUANTIZE = 2048

FLOPS = 2 * K * H * (S + M) + 2 * 2 * H * N * S


def tile_list_perfusion_viability_scorer_kernel(
    tc, tab_words, tab_scales, offs, tab2_words, tab2_scales, offs2, pos1, w1, ga, gb, base, wgs, w2_words, w2_scales, w3, out
):
    nc = tc.nc
    with ExitStack() as ctx:
        keep = ctx.enter_context(tc.tile_pool(name="keep", bufs=1))
        shared = ctx.enter_context(tc.tile_pool(name="shared", bufs=1))
        psum = ctx.enter_context(tc.psum_pool(name="psum", bufs=1))

        def held(shape, dtype, name):
            return keep.tile(shape, dtype, name=name, align_bytes=64)

        def tenant(shape, dtype, tag):
            return shared.tile(shape, dtype, name=tag, tag=tag, align_bytes=64)

        def bank(i):
            return psum.tile([P, BANK], F32, name="bank%d" % i, tag="bank%d" % i)

        def chunk(c):
            return slice(BANK * c, BANK * (c + 1))

        idx = held([P, S // 16], U16, "idx")
        idx2 = held([P, M // 16], U16, "idx2")
        place = held([P, M // 16], U16, "place")
        tab_w = [tenant([P, T], I32, "tab_w%d" % g) for g in range(PASSES)]
        tab2_w = [held([P, T2], I32, "tab2_w%d" % g) for g in range(PASSES)]
        tab_s = held([P, T // 4], I32, "tab_s")
        tab2_s = held([P, T2 // 4], I32, "tab2_s")
        v_w = [held([P, S], U32, "v_w%d" % g) for g in range(PASSES)]
        v2_w = [held([P, M], U32, "v2_w%d" % g) for g in range(PASSES)]
        v_s = held([P, S], U8, "v_s")
        v2_s = held([P, M], U8, "v2_s")
        w1_c = [held([P, PASSES * PASS], U32, "w1_c")]
        w1_s = [held([P, PASSES * PASS], U8, "w1_s%d" % h) for h in range(PASSES)]
        w2_c = held([P, PASSES, 2 * N // 4], I32, "w2_c")
        w2_s = held([P, PASSES, N // 4], I32, "w2_s")
        w3_s = held([P, PASSES * N], U8, "w3_s")
        placed0_s = held([P, S], U8, "placed0_s")
        z0_c = held([P, S], U32, "z0_c")
        z0_s = held([P, S], U8, "z0_s")
        last_c = [held([P, 2 * BANK], U32, "last_c%d" % c) for c in range(CHUNKS)]
        last_s = [held([P, 2 * BANK], U8, "last_s%d" % c) for c in range(CHUNKS)]
        pages = [held([P, S], F32, "page%d" % s) for s in range(SLICES)]
        woven = [held([P, 2 * WOVEN], BF16, "woven%d" % i) for i in range(3)]
        feats = [held([P, S], F32, "feats%d" % i) for i in range(FEATS)]
        ga_sb = held([P, PASSES, PACK], F32, "ga_sb")
        gb_sb = held([P, PASSES, PACK], F32, "gb_sb")
        wgs_early = [held([P, M], F32, "wgs_early%d" % t) for t in range(2)]
        wgs_late = held([P, 2, M], F32, "wgs_late")
        wgs_plane = [wgs_early[0][:], wgs_early[1][:], wgs_late[:, 0, :], wgs_late[:, 1, :]]

        def half(tile, i):
            return tile[:, WOVEN * i : WOVEN * (i + 1)]

        def quadrant(q, rows):
            return slice(QUAD * q, QUAD * q + rows)

        def load_scale_rows(queue, tile, src):
            for q in range(QUADRANTS):
                rows = src[:, SCALE_ROWS * q : SCALE_ROWS * (q + 1), :]
                queue.dma_start(out=tile[quadrant(q, SCALE_ROWS * PASSES), :], in_=rows.bitcast(I32))

        def load_words(tile, src, g):
            nc.sync.dma_start(out=tile[:], in_=src[g].rearrange("p n i -> p (n i)").bitcast(I32))

        def load_rows(tile, src, g):
            nc.sync.dma_start(out=tile[:], in_=src[PASS * g : PASS * (g + 1), :].rearrange("(p t) c -> p t c", t=PACK))

        def load_base(g, planes):
            src = base[PASS * g : PASS * (g + 1), :].rearrange("(p t) m -> p t m", t=PACK)
            nc.sync.dma_start(out=base_sb[g][:, planes, :], in_=src[:, planes, :])

        def gather(dst, window, dtype, offsets):
            nc.vector.tensor_copy(out=dst[:], in_=window[:].bitcast(dtype).indirect(offsets[:]))

        def quantize(codes, scales, src):
            nc.vector.quantize_mx(out=codes.bitcast(FP8X4), scales=scales, in_=src)

        def weave(copy, dst, planes):
            copy(
                out=dst.rearrange("p (c i t) -> p c t i", i=RUN, t=PACK),
                in_=planes.rearrange("p t (c i) -> p c t i", i=RUN),
            )

        def weave_w1(copy, dst, raw, cols):
            copy(
                out=dst.rearrange("p (t m j) -> p m t j", t=PACK, j=PACK)[:, cols],
                in_=raw[:].rearrange("p j (m t) -> p m t j", t=PACK)[:, cols],
            )

        def weave_page(s, dst):
            for c in range(CHUNKS):
                nc.scalar.copy(out=dst[c].rearrange("p (j t) -> p j t", t=PACK)[:, :, s % PACK], in_=pages[s][:, chunk(c)])

        def first_product(acc, s, words, scales, cols):
            h, t = divmod(s, PACK)
            for g in range(PASSES):
                rows = slice(PASS * g + P * t, PASS * g + P * (t + 1))
                nc.tensor.matmul_mx(
                    out=acc[:],
                    lhsT=w1_c[h][:, rows].bitcast(FP8X4),
                    lhsT_scale=w1_s[h][:, rows],
                    rhs=words[g][:, cols].bitcast(FP8X4),
                    rhs_scale=scales[SCALE_ROWS * g :, cols],
                    start=(g == 0),
                    stop=(g == PASSES - 1),
                )

        def place_slice(s, b_sb):
            h, t = divmod(s, PACK)
            acc = bank(s % 2)
            first_product(acc, s, v2_w, v2_s, slice(0, M))
            nc.vector.scalar_tensor_tensor(
                out=b_sb, in0=acc[:], scalar=gb_sb[:, h, t : t + 1], in1=base_sb[h][:, t, :], op0=ALU.mult, op1=ALU.subtract
            )
            nc.vector.tensor_tensor(out=pages[s][:].indirect(place[:]), in0=b_sb, in1=wgs_plane[t], op=ALU.mult)

        def feature_slice(s):
            for c in range(CHUNKS):
                acc = bank(2 + CHUNKS * (s % 3) + c)
                first_product(acc, s, v_w, v_s, chunk(c))
                nc.scalar.activation(out=feats[s % FEATS][:, chunk(c)], in_=acc[:], func=ACT.Tanh)

        def difference(s, cols):
            h, t = divmod(s, PACK)
            nc.vector.scalar_tensor_tensor(
                out=z_planes[h][:, t, cols],
                in0=feats[s % FEATS][:, cols],
                scalar=ga_sb[:, h, t : t + 1],
                in1=pages[s][:, cols],
                op0=ALU.mult,
                op1=ALU.subtract,
            )

        nc.vector.memset(tab2_s[:], 0)
        nc.gpsimd.memset(tab_s[:], 0)
        for page in pages[:PACK]:
            nc.vector.memset(page[:].bitcast(I32), 0)
        nc.vector.memset(w2_s[:], 0)

        wgs_rows = wgs.rearrange("(q t) m -> q t m", t=PACK)
        nc.sync.dma_start(idx2[:], offs2)
        nc.sync.dma_start(place[:], pos1)
        nc.sync.dma_start(out=gb_sb[:], in_=gb.rearrange("(h p t) -> p h t", p=P, t=PACK))
        w1_raw = [[tenant([P, PACK, PASS], F32, "wide%d" % (PASSES * h + g)) for g in range(PASSES)] for h in range(PASSES)]
        for g in range(PASSES):
            load_rows(w1_raw[0][g], w1[:, :PASS], g)
        load_scale_rows(nc.scalar, tab2_s, tab2_scales)
        load_scale_rows(nc.gpsimd, tab_s, tab_scales)
        for g in range(PASSES):
            load_words(tab2_w[g], tab2_words, g)
        base_sb = [tenant([P, PACK, M], F32, "base%d" % g) for g in range(PASSES)]

        def load_plane_operands(t):
            load_base(0, t)
            for q in range(QUADRANTS):
                nc.sync.dma_start(out=wgs_early[t][quadrant(q, QUAD), :], in_=wgs_rows[:, t, :])

        load_plane_operands(0)
        nc.sync.dma_start(idx[:], offs)
        load_rows(w1_raw[1][0], w1[:, PASS:], 0)
        load_plane_operands(1)
        load_rows(w1_raw[1][1], w1[:, PASS:], 1)
        load_base(0, 2)
        for q in range(QUADRANTS):
            nc.sync.dma_start(out=wgs_late[quadrant(q, QUAD)], in_=wgs_rows[:, 2:, :])
        load_base(0, 3)
        w3_raw = [tenant([P, PACK, N], F32, "wide%d" % g) for g in range(PASSES)]
        for g in range(PASSES):
            load_rows(w3_raw[g], w3, g)
        for g in range(PASSES):
            load_words(tab_w[g], tab_words, g)
        load_base(1, 0)
        nc.sync.dma_start(out=ga_sb[:], in_=ga.rearrange("(h p t) -> p h t", p=P, t=PACK))
        load_base(1, slice(1, PACK))
        for q in range(QUADRANTS):
            rows = w2_scales[:, SCALE_ROWS * q : SCALE_ROWS * (q + 1), :].rearrange("g r c -> r g c")
            nc.gpsimd.dma_start(out=w2_s[quadrant(q, SCALE_ROWS)], in_=rows.bitcast(I32))
        nc.sync.dma_start(out=w2_c[:], in_=w2_words.rearrange("g p c -> p g c").bitcast(I32))
        for page in pages[PACK:]:
            nc.gpsimd.memset(page[:].bitcast(I32), 0)

        weave_w1(nc.scalar.copy, half(woven[0], 0), w1_raw[0][0], slice(0, P))
        quantize(w1_c[0][:, :PASS], w1_s[0][:, :PASS], half(woven[0], 0))
        gather(v2_s, tab2_s, U8, idx2)
        weave_w1(nc.scalar.copy, half(woven[0], 1), w1_raw[0][1], slice(0, P // 2))
        weave_w1(nc.vector.tensor_copy, half(woven[0], 1), w1_raw[0][1], slice(P // 2, P))
        quantize(w1_c[0][:, PASS:], w1_s[0][:, PASS:], half(woven[0], 1))
        for g in range(PASSES):
            gather(v2_w[g], tab2_w[g], U32, idx2)
        gather(v_s, tab_s, U8, idx)

        placed0_woven = [half(woven[0], c) for c in range(CHUNKS)]
        for s in range(2):
            place_slice(s, feats[s][:, :M])
            weave_page(s, placed0_woven)
            weave_w1(nc.scalar.copy, half(woven[1], s), w1_raw[1][s], slice(0, P))
        for g in range(PASSES):
            weave(nc.scalar.copy, woven[2][:, N * PACK * g : N * PACK * (g + 1)], w3_raw[g][:])
        for s in range(2, PACK):
            place_slice(s, feats[s][:, :M])
            weave_page(s, placed0_woven)

        gather(v_w[0], tab_w[0], U32, idx)
        w1_c.append(tenant([P, PASSES * PASS], U32, "tab_w0"))
        quantize(w1_c[1][:], w1_s[1][:], woven[1][:])
        gather(v_w[1], tab_w[1], U32, idx)

        b4_sb = tenant([P, M], F32, "late")
        place_slice(PACK, b4_sb[:])
        late_c = tenant([P, S + PASSES * N], U32, "late")
        placed0_c = late_c[:, :S]
        w3_c = late_c[:, S:]
        quantize(placed0_c, placed0_s[:], woven[0][:])
        cut = WIDE_QUANTIZE // PACK
        quantize(w3_c[:, :cut], w3_s[:, :cut], woven[2][:, :WIDE_QUANTIZE])
        quantize(w3_c[:, cut:], w3_s[:, cut:], woven[2][:, WIDE_QUANTIZE : PASSES * N * PACK])

        z_planes = [tenant([P, PACK, S], BF16, "wide%d" % (PASSES + g)) for g in range(PASSES)]
        for s in range(PACK):
            feature_slice(s)
            difference(s, slice(0, S))
        feature_slice(PACK)
        for s in range(PACK + 1, SLICES):
            place_slice(s, feats[(s - 2) % FEATS][:, :M])
            difference(s - 1, slice(0, S))
            feature_slice(s)
        for c in range(CHUNKS):
            weave(nc.scalar.copy, half(woven[1], c), z_planes[0][:, :, chunk(c)])

        last_woven = [woven[2], woven[0]]
        placed1_woven = [half(last_woven[c], 0) for c in range(CHUNKS)]
        pair = tenant([P, 2, S], F32, "base0")
        for t in range(2):
            nc.sync.dma_start(out=pair[:, t, :], in_=pages[PACK + t][:])
        for c in range(CHUNKS):
            nc.scalar.copy(
                out=placed1_woven[c].rearrange("p (j t) -> p j t", t=PACK)[:, :, 0:2],
                in_=pair[:, :, chunk(c)].rearrange("p t j -> p j t"),
            )
        for s in range(PACK + 2, SLICES):
            weave_page(s, placed1_woven)
        for c in range(CHUNKS):
            difference(SLICES - 1, chunk(c))
        for c in range(CHUNKS):
            quantize(z0_c[:, chunk(c)], z0_s[:, chunk(c)], half(woven[1], c))
        quarter = BANK // 2
        z1_woven = [half(last_woven[c], 1) for c in range(CHUNKS)]
        weave(nc.vector.tensor_copy, z1_woven[0], z_planes[1][:, :, chunk(0)])
        weave(nc.scalar.copy, z1_woven[1][:, : quarter * PACK], z_planes[1][:, :, BANK : BANK + quarter])
        for c in range(CHUNKS):
            quantize(last_c[c][:, :BANK], last_s[c][:, :BANK], placed1_woven[c])
        quantize(last_c[0][:, BANK:], last_s[0][:, BANK:], z1_woven[0])
        weave(nc.vector.tensor_copy, z1_woven[1][:, quarter * PACK :], z_planes[1][:, :, BANK + quarter :])
        quantize(last_c[1][:, BANK:], last_s[1][:, BANK:], z1_woven[1])

        w2_codes = w2_c[:].bitcast(U8)
        w2_scale = w2_s[:].bitcast(U8)
        y_banks = [[6, 7, 2], [0, 1, 6]]
        y2_banks = [[3, 4, 5], [7, 2, 3]]
        for c in range(CHUNKS):
            z_ops = [(z0_c[:, chunk(c)], z0_s[:, chunk(c)]), (last_c[c][:, BANK:], last_s[c][:, BANK:])]
            placed_ops = [(placed0_c[:, chunk(c)], placed0_s[:, chunk(c)]), (last_c[c][:, :BANK], last_s[c][:, :BANK])]
            res = tenant([P, OUT_SLICES, BANK], F32, "base%d" % c)
            y = [bank(i) for i in y_banks[c]]
            y2 = [bank(i) for i in y2_banks[c]]
            for g in range(PASSES):
                for n in range(OUT_SLICES):
                    w3_cols = slice(N * g + P * n, N * g + P * (n + 1))
                    nc.tensor.matmul_mx(
                        out=y[n][:],
                        lhsT=w2_codes[:, g, 2 * P * n : 2 * P * (n + 1)].bitcast(FP4X4),
                        lhsT_scale=w2_scale[:, g, P * n : P * (n + 1)],
                        rhs=z_ops[g][0].bitcast(FP8X4),
                        rhs_scale=z_ops[g][1],
                        start=(g == 0),
                        stop=(g == PASSES - 1),
                    )
                    nc.tensor.matmul_mx(
                        out=y2[n][:],
                        lhsT=w3_c[:, w3_cols].bitcast(FP8X4),
                        lhsT_scale=w3_s[:, w3_cols],
                        rhs=placed_ops[g][0].bitcast(FP8X4),
                        rhs_scale=placed_ops[g][1],
                        start=(g == 0),
                        stop=(g == PASSES - 1),
                    )
            for n in range(OUT_SLICES):
                nc.scalar.copy(out=res[:, n, :], in_=y[n][:])
                nc.vector.tensor_tensor(out=res[:, n, :], in0=y2[n][:], in1=res[:, n, :], op=ALU.max)
                nc.sync.dma_start(out=out[P * n : P * (n + 1), chunk(c)], in_=res[:, n, :])
